import numpy as np, ml_dtypes
CORES = [8,136,40,168]
N = 4
import mx_ref
NC, G = 256, 4
EPS = 0.001
BF = ml_dtypes.bfloat16
def cut(t, i, w=512):
    return t[:, w * i:w * i + w]
def tile(rs):
    return np.stack(rs, axis=2).reshape(128, -1).astype(BF)
def layer(w, X):
    out = []
    for i in range(G):
        for t in range(len(X)):
            p = mx_ref.matmul(mx_ref.quantize(cut(w, len(X) * i + t)), X[t])
            z = p if t == 0 else z + p
        out.append(z)
    return out
def setup_inputs(rng):
    def f(*shape):
        return mx_ref.flush((rng.standard_normal(shape, dtype=np.float32) * np.exp2(rng.integers(-2, 3, shape[:-1] + (1,)))).astype(BF))
    return {"x": f(N, 128, 4 * NC), "w1": f(N, 128, G * 512), "w2": f(N, 128, 2 * 512)}
def setup_inputs_blocks(rng):
    d = setup_inputs(rng)
    for k in ("x", "w1", "w2"): d[k] = mx_ref.spread(d[k], rng, 4)
    return d
def setup_inputs_wide(rng):
    d = setup_inputs(rng)
    for k in ("x", "w1", "w2"): d[k] = mx_ref.flush((d[k].astype(np.float32) * np.exp2(rng.integers(-6, 7, (N, 1, 1))).astype(np.float32)).astype(BF))
    return d
def setup_inputs_cols(rng):
    d = setup_inputs(rng); v = d["x"].astype(np.float32).reshape(N, 128, -1, 4)
    d["x"] = mx_ref.flush((v * np.exp2(rng.integers(-6, 7, (N, 1, v.shape[2], 1))).astype(np.float32)).reshape(d["x"].shape).astype(BF))
    return d
def setup_inputs_faint(rng):
    d = setup_inputs(rng); d["x"] = mx_ref.flush((d["x"].astype(np.float32) * np.float32(2.0 ** -12)).astype(BF))
    return d
def reference(x, w1, w2, own=None):
    h = np.zeros((N, 128, 4 * NC), BF)
    for r in range(N):
        Z = layer(w1[r], [mx_ref.quantize(x[r])]); R = Z
        ms = sum((v.astype(np.float64) ** 2).sum(axis=0) for v in R) / 512
        s = (1 / np.sqrt(ms + EPS)).astype(np.float32)
        h[r] = tile([v * s for v in R])
    use = h if own is None else own["h"]
    H = [mx_ref.quantize(use[j]) for j in range(N)]
    y = np.zeros((N, 128, NC), np.float32)
    for r in range(N):
        y[r] = mx_ref.matmul(mx_ref.quantize(cut(w2[r], 0)), H[r]) + mx_ref.matmul(mx_ref.quantize(cut(w2[r], 1)), H[(r + 1) % N])
    return {"h": h, "y": y}

@@ -1,0 +1,195 @@
+from concourse.mybir import dt, AluOpType, ActivationFunctionType
+
+EPS = 0.001
+NCOL = 256
+HALF = 128
+
+SCRATCH = {
+    "xb": ("sbuf", [128, 1024], "bfloat16"),
+    "w1b": ("sbuf", [128, 2048], "bfloat16"),
+    "w2b": ("sbuf", [128, 1024], "bfloat16"),
+    "hb": ("sbuf", [128, 1024], "bfloat16"),
+    "xq": ("sbuf", [128, 256], "float8_e4m3fn_x4"), "xs": ("sbuf", [128, 256], "uint8"),
+    "w1q": ("sbuf", [128, 512], "float8_e4m3fn_x4"), "w1s": ("sbuf", [128, 512], "uint8"),
+    "w2q": ("sbuf", [128, 256], "float8_e4m3fn_x4"), "w2s": ("sbuf", [128, 256], "uint8"),
+    "hq": ("sbuf", [128, 256], "float8_e4m3fn_x4"), "hs": ("sbuf", [128, 256], "uint8"),
+    "rq": ("sbuf", [128, 256], "float8_e4m3fn_x4"), "rs": ("sbuf", [128, 256], "uint8"),
+    "sq": ("sbuf", [128, 1024], "float32"),
+    "zs": ("sbuf", [128, 1024], "float32"),
+    "ones": ("sbuf", [128, 128], "float32"),
+    "frac": ("sbuf", [128, 4], "float32"),
+    "ident": ("sbuf", [128, 128], "float32"),
+    "dg": ("sbuf", [128, 256], "float32"),
+    "st": ("sbuf", [128, 16], "float32"),
+    "yb": ("sbuf", [128, 256], "float32"),
+    "z": ("psum", [128, 2048], "float32"),
+    "pa": ("psum", [128, 512], "float32"),
+    "pr": ("psum", [128, 1024], "float32"),
+    "pS": ("psum", [128, 512], "float32"),
+}
+SEMAPHORES = (["ldx", "ldv", "ones", "frac", "ident", "qx", "qv", "A", "ra", "a", "k", "k2", "c2", "sent", "hst"]
+              + ["ldw%d" % b for b in range(4)] + ["qw%d" % b for b in range(4)] + ["z%d" % b for b in range(4)]
+              + ["cz0", "cz1", "cz2", "cz3a", "cz3b", "sq0", "sq1", "sq2", "sq3a", "sq3b"]
+              + [n + str(c) for n in ("R", "rq", "iq", "dg", "S", "hm", "qh", "arr", "y", "yc", "st") for c in range(2)])
+
+
+def rank_program(g, core, T, topo):
+    rank = T.rank_of(core)
+    if rank is None:
+        return
+    S, V, A, P, Y = T.sem, g.vector, g.scalar, g.tensor, g.sync
+    AF, OP = ActivationFunctionType, AluOpType
+    n = len(T.cores)
+    dst = T.cores[(rank - 1) % n]
+    rid, pid = topo.addr(dst, core)
+    mask = topo.mask(core, dst)
+    eng = bin(mask).count("1")
+
+    def zb(b, lo=0, hi=NCOL):
+        return T.z[:, 512 * b + lo:512 * b + hi]
+
+    def sb(t, b, lo=0, hi=NCOL):
+        return t[:, NCOL * b + lo:NCOL * b + hi]
+
+    def col(i, c):
+        return T.st[:, 2 * i + c:2 * i + c + 1]
+
+    def pair(i):
+        return T.st[:, 2 * i:2 * i + 2]
+    RA, AA, K, K2, C2, RQ, IQ = range(7)
+
+    Y.dma_start(T.xb[:], T.x[:]).then_inc(S.ldx, 16)
+    A.dma_start(T.w1b[:, 0:512], T.w1[:, 0:512]).then_inc(S.ldw0, 16)
+    Y.dma_start(T.w1b[:, 512:1024], T.w1[:, 512:1024]).then_inc(S.ldw1, 16)
+    A.dma_start(T.w1b[:, 1024:1536], T.w1[:, 1024:1536]).then_inc(S.ldw2, 16)
+    Y.dma_start(T.w1b[:, 1536:2048], T.w1[:, 1536:2048]).then_inc(S.ldw3, 16)
+    A.dma_start(T.w2b[:], T.w2[:]).then_inc(S.ldv, 16)
+
+    V.memset(T.ones[:], 1.0).then_inc(S.ones, 1)
+    V.memset(T.frac[:], 1.0 / 512.0).then_inc(S.frac, 1)
+    V.wait_ge(S.ldx, 16)
+    V.quantize_mx(T.xq[:], T.xs[:], T.xb[:]).then_inc(S.qx, 1)
+
+    def quant_w1(b):
+        V.wait_ge(S["ldw%d" % b], 16)
+        V.quantize_mx(T.w1q[:, 128 * b:128 * b + 128], T.w1s[:, 128 * b:128 * b + 128],
+                      T.w1b[:, 512 * b:512 * b + 512]).then_inc(S["qw%d" % b], 1)
+    quant_w1(0)
+    quant_w1(1)
+    quant_w1(2)
+    for b in (0, 1):
+        V.wait_ge(S["sq%d" % b], 1)
+        V.tensor_copy(sb(T.zs, b), zb(b)).then_inc(S["cz%d" % b], 1)
+    quant_w1(3)
+    V.wait_ge(S.z2, 1)
+    V.tensor_copy(sb(T.zs, 2), zb(2)).then_inc(S.cz2, 1)
+    V.wait_ge(S.cz2, 1)
+    V.tensor_tensor(sb(T.sq, 2), zb(2), sb(T.zs, 2), OP.mult).then_inc(S.sq2, 1)
+    V.wait_ge(S.z3, 1)
+    for c, t in ((0, "a"), (1, "b")):
+        lo, hi = HALF * c, HALF * c + HALF
+        V.tensor_copy(sb(T.zs, 3, lo, hi), zb(3, lo, hi)).then_inc(S["cz3" + t], 1)
+        V.wait_ge(S["cz3" + t], 1)
+        V.tensor_tensor(sb(T.sq, 3, lo, hi), zb(3, lo, hi), sb(T.zs, 3, lo, hi), OP.mult).then_inc(S["sq3" + t], 1)
+    V.wait_ge(S.ra, 1)
+    V.reciprocal(pair(K), pair(RA)).then_inc(S.k, 1)
+    V.wait_ge(S.k, 1)
+    V.tensor_tensor(pair(K2), pair(K), pair(K), OP.mult).then_inc(S.k2, 1)
+    V.wait_ge(S.k2, 1)
+    V.wait_ge(S.a, 1)
+    V.tensor_tensor(pair(C2), pair(AA), pair(K2), OP.mult).then_inc(S.c2, 1)
+    V.wait_ge(S.ident, 1)
+    for c in range(2):
+        V.wait_ge(S["rq%d" % c], 1)
+        V.reciprocal(col(IQ, c), col(RQ, c)).then_inc(S["iq%d" % c], 1)
+        V.wait_ge(S["iq%d" % c], 1)
+        V.tensor_scalar(T.dg[:, HALF * c:HALF * c + HALF], T.ident[:], col(IQ, c), col(K, c),
+                        OP.mult, OP.mult).then_inc(S["dg%d" % c], 1)
+    for c in range(2):
+        lo, hi = HALF * c, HALF * c + HALF
+        scales = (T.pS if c == 0 else T.pa)[:, 0:HALF]
+        V.wait_ge(S["S%d" % c], 1)
+        for b in range(4):
+            V.tensor_tensor(T.hb[:, 4 * lo + b:4 * hi:4], sb(T.zs, b, lo, hi), scales, OP.mult).then_inc(S["hm%d" % c], 1)
+        V.wait_ge(S["hm%d" % c], 4)
+        V.quantize_mx(T.hq[:, lo:hi], T.hs[:, lo:hi], T.hb[:, 4 * lo:4 * hi]).then_inc(S["qh%d" % c], 1)
+    V.wait_ge(S.ldv, 16)
+    V.quantize_mx(T.w2q[:], T.w2s[:], T.w2b[:]).then_inc(S.qv, 1)
+
+    def layer1(b):
+        P.wait_ge(S["qw%d" % b], 1)
+        P.matmul_mx(zb(b), T.w1q[:, 128 * b:128 * b + 128], T.w1s[:, 128 * b:128 * b + 128],
+                    T.xq[:], T.xs[:], True, True).then_inc(S["z%d" % b], 1)
+
+    def colsum(out, b, c, start, stop):
+        return P.matmul(out, sb(T.sq, b, HALF * c, HALF * c + HALF), T.frac[:, 0:1], start, stop)
+    P.wait_ge(S.qx, 1)
+    layer1(0)
+    layer1(1)
+    P.wait_ge(S.frac, 1)
+    P.wait_ge(S.sq0, 1)
+    for c in range(2):
+        colsum(T.pa[:, c:c + 1], 0, c, True, True).then_inc(S.A, 1)
+    layer1(2)
+    P.wait_ge(S.sq1, 1)
+    for c in range(2):
+        colsum(T.pr[:, 512 * c:512 * c + 1], 1, c, True, False)
+    layer1(3)
+    P.wait_ge(S.sq2, 1)
+    for c in range(2):
+        colsum(T.pr[:, 512 * c:512 * c + 1], 2, c, False, False)
+    for c, t in ((0, "a"), (1, "b")):
+        P.wait_ge(S["sq3" + t], 1)
+        colsum(T.pr[:, 512 * c:512 * c + 1], 3, c, False, True).then_inc(S["R%d" % c], 1)
+    P.wait_ge(S.ones, 1)
+    P.wait_ge(S.ra, 1)
+    P.wait_ge(S.a, 1)
+    for c in range(2):
+        P.wait_ge(S["dg%d" % c], 1)
+        P.matmul((T.pS if c == 0 else T.pa)[:, 0:HALF], T.ones[:], T.dg[:, HALF * c:HALF * c + HALF],
+                 True, True).then_inc(S["S%d" % c], 1)
+    P.wait_ge(S.qv, 1)
+    for c in range(2):
+        P.wait_ge(S["cz%d" % c], 1)
+        P.wait_ge(S["qh%d" % c], 1)
+        P.matmul_mx(zb(c, 0, HALF), T.w2q[:, 0:128], T.w2s[:, 0:128],
+                    T.hq[:, HALF * c:HALF * c + HALF], T.hs[:, HALF * c:HALF * c + HALF], True, False)
+    for c in range(2):
+        P.wait_ge(S["arr%d" % c], 2 * eng)
+        P.matmul_mx(zb(c, 0, HALF), T.w2q[:, 128:256], T.w2s[:, 128:256],
+                    T.rq[:, HALF * c:HALF * c + HALF], T.rs[:, HALF * c:HALF * c + HALF], False, True).then_inc(S["y%d" % c], 1)
+
+    for b in (0, 1):
+        A.wait_ge(S["z%d" % b], 1)
+        A.activation(sb(T.sq, b), zb(b), AF.Square).then_inc(S["sq%d" % b], 1)
+    A.wait_ge(S.A, 2)
+    A.activation(pair(RA), T.pa[:, 0:2], AF.Sqrt, bias=EPS).then_inc(S.ra, 1)
+    A.activation(pair(AA), T.pa[:, 0:2], AF.Identity, bias=EPS).then_inc(S.a, 1)
+    A.wait_ge(S.k2, 1)
+    A.wait_ge(S.c2, 1)
+    for c in range(2):
+        A.wait_ge(S["R%d" % c], 1)
+        A.activation(col(RQ, c), T.pr[:, 512 * c:512 * c + 1], AF.Sqrt, bias=col(C2, c), scale=col(K2, c)).then_inc(S["rq%d" % c], 1)
+    for c in range(2):
+        lo, hi = HALF * c, HALF * c + HALF
+        A.wait_ge(S["y%d" % c], 1)
+        A.activation(T.yb[:, lo:hi], zb(c, 0, HALF), AF.Copy).then_inc(S["yc%d" % c], 1)
+        A.wait_ge(S["yc%d" % c], 1)
+        A.dma_start(T.y[:, lo:hi], T.yb[:, lo:hi]).then_inc(S["st%d" % c], 16)
+    A.wait_ge(S.st0, 16)
+    A.wait_ge(S.st1, 16)
+
+    g.wait_ge(S.ones, 1)
+    g.affine_select(T.ident[:], T.ones[:], [[-1, 128]], OP.is_equal, 0.0, 0, 1).then_inc(S.ident, 1)
+    for c in range(2):
+        lo, hi = HALF * c, HALF * c + HALF
+        g.wait_ge(S["qh%d" % c], 1)
+        g.remote_dma(T.rq[:, lo:hi].bitcast(dt.uint8), T.hq[:, lo:hi].bitcast(dt.uint8), S["arr%d" % c], S.sent, pid, rid, mask)
+        g.remote_dma(T.rs[:, lo:hi], T.hs[:, lo:hi], S["arr%d" % c], S.sent, pid, rid, mask)
+    g.wait_ge(S.sent, 4 * eng)
+
+    Y.wait_ge(S.hm0, 4)
+    Y.wait_ge(S.hm1, 4)
+    Y.wait_ge(S.sent, 4 * eng)
+    Y.dma_start(T.h[:], T.hb[:]).then_inc(S.hst, 16)
+    Y.wait_ge(S.hst, 16)

@@ -3,6 +3,7 @@ from concourse.mybir import dt, AluOpType, ActivationFunctionType
 EPS = 0.001
 NCOL = 256
 HALF = 128
+PIECE = 64
 
 SCRATCH = {
     "xb": ("sbuf", [128, 1024], "bfloat16"),
@@ -20,6 +21,7 @@ SCRATCH = {
     "frac": ("sbuf", [128, 4], "float32"),
     "ident": ("sbuf", [128, 128], "float32"),
     "dg": ("sbuf", [128, 256], "float32"),
+    "idk": ("sbuf", [128, 128], "float32"),
     "st": ("sbuf", [128, 16], "float32"),
     "yb": ("sbuf", [128, 256], "float32"),
     "z": ("psum", [128, 2048], "float32"),
@@ -27,10 +29,10 @@ SCRATCH = {
     "pr": ("psum", [128, 1024], "float32"),
     "pS": ("psum", [128, 512], "float32"),
 }
-SEMAPHORES = (["ldx", "ldv", "ones", "frac", "ident", "qx", "qv", "A", "ra", "a", "k", "k2", "c2", "sent", "hst"]
-              + ["ldw%d" % b for b in range(4)] + ["qw%d" % b for b in range(4)] + ["z%d" % b for b in range(4)]
+SEMAPHORES = (["ldx", "ldv", "ones", "frac", "ident", "qx", "qv", "A", "ra", "a", "k", "k2", "c2", "sent", "hst", "idk"]
+              + ["ldw%d" % b for b in range(4)] + ["qw%d" % b for b in range(4)] + ["z0", "z1", "z2", "z3a", "z3b"]
               + ["cz0", "cz1", "cz2", "cz3a", "cz3b", "sq0", "sq1", "sq2", "sq3a", "sq3b"]
-              + [n + str(c) for n in ("R", "rq", "iq", "dg", "S", "hm", "qh", "arr", "y", "yc", "st") for c in range(2)])
+              + [n + str(c) for n in ("R", "rq", "iq", "hm", "qh", "arr", "y", "yc", "st", "dg0", "dg1", "S0", "S1") for c in range(2)])
 
 
 def rank_program(g, core, T, topo):
@@ -44,9 +46,16 @@ def rank_program(g, core, T, topo):
     rid, pid = topo.addr(dst, core)
     mask = topo.mask(core, dst)
     eng = bin(mask).count("1")
+    HALVES = ((0, "a"), (1, "b"))
 
     def zb(b, lo=0, hi=NCOL):
         return T.z[:, 512 * b + lo:512 * b + hi]
+
+    def z3(c):
+        return T.z[:, 1536:1536 + HALF] if c == 0 else T.pa[:, 0:HALF]
+
+    def scal(c, q):
+        return (T.pS[:, 0:PIECE], T.z[:, 1024:1024 + PIECE], T.z[:, 1536:1536 + PIECE], T.pa[:, 0:PIECE])[2 * c + q]
 
     def sb(t, b, lo=0, hi=NCOL):
         return t[:, NCOL * b + lo:NCOL * b + hi]
@@ -63,7 +72,8 @@ def rank_program(g, core, T, topo):
     Y.dma_start(T.w1b[:, 512:1024], T.w1[:, 512:1024]).then_inc(S.ldw1, 16)
     A.dma_start(T.w1b[:, 1024:1536], T.w1[:, 1024:1536]).then_inc(S.ldw2, 16)
     Y.dma_start(T.w1b[:, 1536:2048], T.w1[:, 1536:2048]).then_inc(S.ldw3, 16)
-    A.dma_start(T.w2b[:], T.w2[:]).then_inc(S.ldv, 16)
+    Y.wait_ge(S.ldw3, 16)
+    Y.dma_start(T.w2b[:], T.w2[:]).then_inc(S.ldv, 16)
 
     V.memset(T.ones[:], 1.0).then_inc(S.ones, 1)
     V.memset(T.frac[:], 1.0 / 512.0).then_inc(S.frac, 1)
@@ -77,20 +87,13 @@ def rank_program(g, core, T, topo):
     quant_w1(0)
     quant_w1(1)
     quant_w1(2)
-    for b in (0, 1):
-        V.wait_ge(S["sq%d" % b], 1)
-        V.tensor_copy(sb(T.zs, b), zb(b)).then_inc(S["cz%d" % b], 1)
-    quant_w1(3)
+    V.wait_ge(S.sq1, 1)
+    V.tensor_copy(sb(T.zs, 1), zb(1)).then_inc(S.cz1, 1)
     V.wait_ge(S.z2, 1)
     V.tensor_copy(sb(T.zs, 2), zb(2)).then_inc(S.cz2, 1)
     V.wait_ge(S.cz2, 1)
     V.tensor_tensor(sb(T.sq, 2), zb(2), sb(T.zs, 2), OP.mult).then_inc(S.sq2, 1)
-    V.wait_ge(S.z3, 1)
-    for c, t in ((0, "a"), (1, "b")):
-        lo, hi = HALF * c, HALF * c + HALF
-        V.tensor_copy(sb(T.zs, 3, lo, hi), zb(3, lo, hi)).then_inc(S["cz3" + t], 1)
-        V.wait_ge(S["cz3" + t], 1)
-        V.tensor_tensor(sb(T.sq, 3, lo, hi), zb(3, lo, hi), sb(T.zs, 3, lo, hi), OP.mult).then_inc(S["sq3" + t], 1)
+    quant_w1(3)
     V.wait_ge(S.ra, 1)
     V.reciprocal(pair(K), pair(RA)).then_inc(S.k, 1)
     V.wait_ge(S.k, 1)
@@ -98,20 +101,28 @@ def rank_program(g, core, T, topo):
     V.wait_ge(S.k2, 1)
     V.wait_ge(S.a, 1)
     V.tensor_tensor(pair(C2), pair(AA), pair(K2), OP.mult).then_inc(S.c2, 1)
+    for c, t in HALVES:
+        V.wait_ge(S["sq3" + t], 1)
+        V.tensor_copy(sb(T.zs, 3, HALF * c, HALF * c + HALF), z3(c)).then_inc(S["cz3" + t], 1)
     V.wait_ge(S.ident, 1)
-    for c in range(2):
-        V.wait_ge(S["rq%d" % c], 1)
-        V.reciprocal(col(IQ, c), col(RQ, c)).then_inc(S["iq%d" % c], 1)
-        V.wait_ge(S["iq%d" % c], 1)
-        V.tensor_scalar(T.dg[:, HALF * c:HALF * c + HALF], T.ident[:], col(IQ, c), col(K, c),
-                        OP.mult, OP.mult).then_inc(S["dg%d" % c], 1)
+    V.wait_ge(S.rq0, 1)
+    V.reciprocal(col(IQ, 0), col(RQ, 0)).then_inc(S.iq0, 1)
+    V.wait_ge(S.iq0, 1)
+    for q in range(2):
+        V.tensor_scalar(T.dg[:, PIECE * q:PIECE * q + PIECE], T.ident[:, PIECE * q:PIECE * q + PIECE], col(IQ, 0), col(K, 0),
+                        OP.mult, OP.mult).then_inc(S["dg0%d" % q], 1)
+    V.wait_ge(S.rq1, 1)
+    V.reciprocal(col(IQ, 1), col(RQ, 1)).then_inc(S.iq1, 1)
+    for name in ("cz0", "cz1", "cz3a", "cz3b"):
+        V.wait_ge(S[name], 1)
     for c in range(2):
         lo, hi = HALF * c, HALF * c + HALF
-        scales = (T.pS if c == 0 else T.pa)[:, 0:HALF]
-        V.wait_ge(S["S%d" % c], 1)
-        for b in range(4):
-            V.tensor_tensor(T.hb[:, 4 * lo + b:4 * hi:4], sb(T.zs, b, lo, hi), scales, OP.mult).then_inc(S["hm%d" % c], 1)
-        V.wait_ge(S["hm%d" % c], 4)
+        for q in range(2):
+            pl, ph = lo + PIECE * q, lo + PIECE * q + PIECE
+            V.wait_ge(S["S%d%d" % (c, q)], 1)
+            for b in range(4):
+                V.tensor_tensor(T.hb[:, 4 * pl + b:4 * ph:4], sb(T.zs, b, pl, ph), scal(c, q), OP.mult).then_inc(S["hm%d" % c], 1)
+        V.wait_ge(S["hm%d" % c], 8)
         V.quantize_mx(T.hq[:, lo:hi], T.hs[:, lo:hi], T.hb[:, 4 * lo:4 * hi]).then_inc(S["qh%d" % c], 1)
     V.wait_ge(S.ldv, 16)
     V.quantize_mx(T.w2q[:], T.w2s[:], T.w2b[:]).then_inc(S.qv, 1)
@@ -129,25 +140,32 @@ def rank_program(g, core, T, topo):
     P.wait_ge(S.frac, 1)
     P.wait_ge(S.sq0, 1)
     for c in range(2):
-        colsum(T.pa[:, c:c + 1], 0, c, True, True).then_inc(S.A, 1)
+        colsum(T.pS[:, c:c + 1], 0, c, True, True).then_inc(S.A, 1)
     layer1(2)
     P.wait_ge(S.sq1, 1)
     for c in range(2):
         colsum(T.pr[:, 512 * c:512 * c + 1], 1, c, True, False)
-    layer1(3)
     P.wait_ge(S.sq2, 1)
     for c in range(2):
         colsum(T.pr[:, 512 * c:512 * c + 1], 2, c, False, False)
-    for c, t in ((0, "a"), (1, "b")):
+    P.wait_ge(S.qw3, 1)
+    for c, t in HALVES:
+        P.matmul_mx(z3(c), T.w1q[:, 384:512], T.w1s[:, 384:512], T.xq[:, HALF * c:HALF * c + HALF],
+                    T.xs[:, HALF * c:HALF * c + HALF], True, True).then_inc(S["z3" + t], 1)
+    for c, t in HALVES:
         P.wait_ge(S["sq3" + t], 1)
         colsum(T.pr[:, 512 * c:512 * c + 1], 3, c, False, True).then_inc(S["R%d" % c], 1)
     P.wait_ge(S.ones, 1)
     P.wait_ge(S.ra, 1)
     P.wait_ge(S.a, 1)
+    P.wait_ge(S.cz2, 1)
+    P.wait_ge(S.cz3a, 1)
+    P.wait_ge(S.cz3b, 1)
     for c in range(2):
-        P.wait_ge(S["dg%d" % c], 1)
-        P.matmul((T.pS if c == 0 else T.pa)[:, 0:HALF], T.ones[:], T.dg[:, HALF * c:HALF * c + HALF],
-                 True, True).then_inc(S["S%d" % c], 1)
+        for q in range(2):
+            lo = HALF * c + PIECE * q
+            P.wait_ge(S["dg%d%d" % (c, q)], 1)
+            P.matmul(scal(c, q), T.ones[:], T.dg[:, lo:lo + PIECE], True, True).then_inc(S["S%d%d" % (c, q)], 1)
     P.wait_ge(S.qv, 1)
     for c in range(2):
         P.wait_ge(S["cz%d" % c], 1)
@@ -159,17 +177,30 @@ def rank_program(g, core, T, topo):
         P.matmul_mx(zb(c, 0, HALF), T.w2q[:, 128:256], T.w2s[:, 128:256],
                     T.rq[:, HALF * c:HALF * c + HALF], T.rs[:, HALF * c:HALF * c + HALF], False, True).then_inc(S["y%d" % c], 1)
 
-    for b in (0, 1):
-        A.wait_ge(S["z%d" % b], 1)
-        A.activation(sb(T.sq, b), zb(b), AF.Square).then_inc(S["sq%d" % b], 1)
+    A.wait_ge(S.z0, 1)
+    A.activation(sb(T.sq, 0), zb(0), AF.Square).then_inc(S.sq0, 1)
+    A.activation(sb(T.zs, 0), zb(0), AF.Copy).then_inc(S.cz0, 1)
+    A.wait_ge(S.z1, 1)
+    A.activation(sb(T.sq, 1), zb(1), AF.Square).then_inc(S.sq1, 1)
     A.wait_ge(S.A, 2)
-    A.activation(pair(RA), T.pa[:, 0:2], AF.Sqrt, bias=EPS).then_inc(S.ra, 1)
-    A.activation(pair(AA), T.pa[:, 0:2], AF.Identity, bias=EPS).then_inc(S.a, 1)
+    A.activation(pair(RA), T.pS[:, 0:2], AF.Sqrt, bias=EPS).then_inc(S.ra, 1)
+    A.activation(pair(AA), T.pS[:, 0:2], AF.Identity, bias=EPS).then_inc(S.a, 1)
+    for c, t in HALVES:
+        A.wait_ge(S["z3" + t], 1)
+        A.activation(sb(T.sq, 3, HALF * c, HALF * c + HALF), z3(c), AF.Square).then_inc(S["sq3" + t], 1)
+    A.wait_ge(S.k, 1)
+    A.wait_ge(S.ident, 1)
+    A.activation(T.idk[:], T.ident[:], AF.Identity, scale=col(K, 1)).then_inc(S.idk, 1)
     A.wait_ge(S.k2, 1)
     A.wait_ge(S.c2, 1)
     for c in range(2):
         A.wait_ge(S["R%d" % c], 1)
         A.activation(col(RQ, c), T.pr[:, 512 * c:512 * c + 1], AF.Sqrt, bias=col(C2, c), scale=col(K2, c)).then_inc(S["rq%d" % c], 1)
+    A.wait_ge(S.idk, 1)
+    A.wait_ge(S.iq1, 1)
+    for q in range(2):
+        A.activation(T.dg[:, HALF + PIECE * q:HALF + PIECE * q + PIECE], T.idk[:, PIECE * q:PIECE * q + PIECE], AF.Identity,
+                     scale=col(IQ, 1)).then_inc(S["dg1%d" % q], 1)
     for c in range(2):
         lo, hi = HALF * c, HALF * c + HALF
         A.wait_ge(S["y%d" % c], 1)
@@ -188,8 +219,8 @@ def rank_program(g, core, T, topo):
         g.remote_dma(T.rs[:, lo:hi], T.hs[:, lo:hi], S["arr%d" % c], S.sent, pid, rid, mask)
     g.wait_ge(S.sent, 4 * eng)
 
-    Y.wait_ge(S.hm0, 4)
-    Y.wait_ge(S.hm1, 4)
+    Y.wait_ge(S.hm0, 8)
+    Y.wait_ge(S.hm1, 8)
     Y.wait_ge(S.sent, 4 * eng)
     Y.dma_start(T.h[:], T.hb[:]).then_inc(S.hst, 16)
     Y.wait_ge(S.hst, 16)

from concourse.mybir import dt, AluOpType, ActivationFunctionType

EPS = 0.001
NCOL = 256
HALF = 128
PIECE = 64

SCRATCH = {
    "xb": ("sbuf", [128, 1024], "bfloat16"),
    "w1b": ("sbuf", [128, 2048], "bfloat16"),
    "w2b": ("sbuf", [128, 1024], "bfloat16"),
    "hb": ("sbuf", [128, 1024], "bfloat16"),
    "xq": ("sbuf", [128, 256], "float8_e4m3fn_x4"), "xs": ("sbuf", [128, 256], "uint8"),
    "w1q": ("sbuf", [128, 512], "float8_e4m3fn_x4"), "w1s": ("sbuf", [128, 512], "uint8"),
    "w2q": ("sbuf", [128, 256], "float8_e4m3fn_x4"), "w2s": ("sbuf", [128, 256], "uint8"),
    "hq": ("sbuf", [128, 256], "float8_e4m3fn_x4"), "hs": ("sbuf", [128, 256], "uint8"),
    "rq": ("sbuf", [128, 256], "float8_e4m3fn_x4"), "rs": ("sbuf", [128, 256], "uint8"),
    "sq": ("sbuf", [128, 1024], "float32"),
    "zs": ("sbuf", [128, 1024], "float32"),
    "ones": ("sbuf", [128, 128], "float32"),
    "frac": ("sbuf", [128, 4], "float32"),
    "ident": ("sbuf", [128, 128], "float32"),
    "dg": ("sbuf", [128, 256], "float32"),
    "idk": ("sbuf", [128, 128], "float32"),
    "st": ("sbuf", [128, 16], "float32"),
    "yb": ("sbuf", [128, 256], "float32"),
    "z": ("psum", [128, 2048], "float32"),
    "pa": ("psum", [128, 512], "float32"),
    "pr": ("psum", [128, 1024], "float32"),
    "pS": ("psum", [128, 512], "float32"),
}
SEMAPHORES = (["ldx", "ldv", "ones", "frac", "ident", "qx", "qv", "A", "ra", "a", "k", "k2", "c2", "sent", "hst", "idk"]
              + ["ldw%d" % b for b in range(4)] + ["qw%d" % b for b in range(4)] + ["z0", "z1", "z2", "z3a", "z3b"]
              + ["cz0", "cz1", "cz2", "cz3a", "cz3b", "sq0", "sq1", "sq2", "sq3a", "sq3b"]
              + [n + str(c) for n in ("R", "rq", "iq", "hm", "qh", "arr", "y", "yc", "st", "dg0", "dg1", "S0", "S1") for c in range(2)])


def rank_program(g, core, T, topo):
    rank = T.rank_of(core)
    if rank is None:
        return
    S, V, A, P, Y = T.sem, g.vector, g.scalar, g.tensor, g.sync
    AF, OP = ActivationFunctionType, AluOpType
    n = len(T.cores)
    dst = T.cores[(rank - 1) % n]
    rid, pid = topo.addr(dst, core)
    mask = topo.mask(core, dst)
    eng = bin(mask).count("1")
    HALVES = ((0, "a"), (1, "b"))

    def zb(b, lo=0, hi=NCOL):
        return T.z[:, 512 * b + lo:512 * b + hi]

    def z3(c):
        return T.z[:, 1536:1536 + HALF] if c == 0 else T.pa[:, 0:HALF]

    def scal(c, q):
        return (T.pS[:, 0:PIECE], T.z[:, 1024:1024 + PIECE], T.z[:, 1536:1536 + PIECE], T.pa[:, 0:PIECE])[2 * c + q]

    def sb(t, b, lo=0, hi=NCOL):
        return t[:, NCOL * b + lo:NCOL * b + hi]

    def col(i, c):
        return T.st[:, 2 * i + c:2 * i + c + 1]

    def pair(i):
        return T.st[:, 2 * i:2 * i + 2]
    RA, AA, K, K2, C2, RQ, IQ = range(7)

    Y.dma_start(T.xb[:], T.x[:]).then_inc(S.ldx, 16)
    A.dma_start(T.w1b[:, 0:512], T.w1[:, 0:512]).then_inc(S.ldw0, 16)
    Y.dma_start(T.w1b[:, 512:1024], T.w1[:, 512:1024]).then_inc(S.ldw1, 16)
    A.dma_start(T.w1b[:, 1024:1536], T.w1[:, 1024:1536]).then_inc(S.ldw2, 16)
    Y.dma_start(T.w1b[:, 1536:2048], T.w1[:, 1536:2048]).then_inc(S.ldw3, 16)
    Y.wait_ge(S.ldw3, 16)
    Y.dma_start(T.w2b[:], T.w2[:]).then_inc(S.ldv, 16)

    V.memset(T.ones[:], 1.0).then_inc(S.ones, 1)
    V.memset(T.frac[:], 1.0 / 512.0).then_inc(S.frac, 1)
    V.wait_ge(S.ldx, 16)
    V.quantize_mx(T.xq[:], T.xs[:], T.xb[:]).then_inc(S.qx, 1)

    def quant_w1(b):
        V.wait_ge(S["ldw%d" % b], 16)
        V.quantize_mx(T.w1q[:, 128 * b:128 * b + 128], T.w1s[:, 128 * b:128 * b + 128],
                      T.w1b[:, 512 * b:512 * b + 512]).then_inc(S["qw%d" % b], 1)
    quant_w1(0)
    quant_w1(1)
    quant_w1(2)
    V.wait_ge(S.sq1, 1)
    V.tensor_copy(sb(T.zs, 1), zb(1)).then_inc(S.cz1, 1)
    V.wait_ge(S.z2, 1)
    V.tensor_copy(sb(T.zs, 2), zb(2)).then_inc(S.cz2, 1)
    V.wait_ge(S.cz2, 1)
    V.tensor_tensor(sb(T.sq, 2), zb(2), sb(T.zs, 2), OP.mult).then_inc(S.sq2, 1)
    quant_w1(3)
    V.wait_ge(S.ra, 1)
    V.reciprocal(pair(K), pair(RA)).then_inc(S.k, 1)
    V.wait_ge(S.k, 1)
    V.tensor_tensor(pair(K2), pair(K), pair(K), OP.mult).then_inc(S.k2, 1)
    V.wait_ge(S.k2, 1)
    V.wait_ge(S.a, 1)
    V.tensor_tensor(pair(C2), pair(AA), pair(K2), OP.mult).then_inc(S.c2, 1)
    for c, t in HALVES:
        V.wait_ge(S["sq3" + t], 1)
        V.tensor_copy(sb(T.zs, 3, HALF * c, HALF * c + HALF), z3(c)).then_inc(S["cz3" + t], 1)
    V.wait_ge(S.ident, 1)
    V.wait_ge(S.rq0, 1)
    V.reciprocal(col(IQ, 0), col(RQ, 0)).then_inc(S.iq0, 1)
    V.wait_ge(S.iq0, 1)
    for q in range(2):
        V.tensor_scalar(T.dg[:, PIECE * q:PIECE * q + PIECE], T.ident[:, PIECE * q:PIECE * q + PIECE], col(IQ, 0), col(K, 0),
                        OP.mult, OP.mult).then_inc(S["dg0%d" % q], 1)
    V.wait_ge(S.rq1, 1)
    V.reciprocal(col(IQ, 1), col(RQ, 1)).then_inc(S.iq1, 1)
    for name in ("cz0", "cz1", "cz3a", "cz3b"):
        V.wait_ge(S[name], 1)
    for c in range(2):
        lo, hi = HALF * c, HALF * c + HALF
        for q in range(2):
            pl, ph = lo + PIECE * q, lo + PIECE * q + PIECE
            V.wait_ge(S["S%d%d" % (c, q)], 1)
            for b in range(4):
                V.tensor_tensor(T.hb[:, 4 * pl + b:4 * ph:4], sb(T.zs, b, pl, ph), scal(c, q), OP.mult).then_inc(S["hm%d" % c], 1)
        V.wait_ge(S["hm%d" % c], 8)
        V.quantize_mx(T.hq[:, lo:hi], T.hs[:, lo:hi], T.hb[:, 4 * lo:4 * hi]).then_inc(S["qh%d" % c], 1)
    V.wait_ge(S.ldv, 16)
    V.quantize_mx(T.w2q[:], T.w2s[:], T.w2b[:]).then_inc(S.qv, 1)

    def layer1(b):
        P.wait_ge(S["qw%d" % b], 1)
        P.matmul_mx(zb(b), T.w1q[:, 128 * b:128 * b + 128], T.w1s[:, 128 * b:128 * b + 128],
                    T.xq[:], T.xs[:], True, True).then_inc(S["z%d" % b], 1)

    def colsum(out, b, c, start, stop):
        return P.matmul(out, sb(T.sq, b, HALF * c, HALF * c + HALF), T.frac[:, 0:1], start, stop)
    P.wait_ge(S.qx, 1)
    layer1(0)
    layer1(1)
    P.wait_ge(S.frac, 1)
    P.wait_ge(S.sq0, 1)
    for c in range(2):
        colsum(T.pS[:, c:c + 1], 0, c, True, True).then_inc(S.A, 1)
    layer1(2)
    P.wait_ge(S.sq1, 1)
    for c in range(2):
        colsum(T.pr[:, 512 * c:512 * c + 1], 1, c, True, False)
    P.wait_ge(S.sq2, 1)
    for c in range(2):
        colsum(T.pr[:, 512 * c:512 * c + 1], 2, c, False, False)
    P.wait_ge(S.qw3, 1)
    for c, t in HALVES:
        P.matmul_mx(z3(c), T.w1q[:, 384:512], T.w1s[:, 384:512], T.xq[:, HALF * c:HALF * c + HALF],
                    T.xs[:, HALF * c:HALF * c + HALF], True, True).then_inc(S["z3" + t], 1)
    for c, t in HALVES:
        P.wait_ge(S["sq3" + t], 1)
        colsum(T.pr[:, 512 * c:512 * c + 1], 3, c, False, True).then_inc(S["R%d" % c], 1)
    P.wait_ge(S.ones, 1)
    P.wait_ge(S.ra, 1)
    P.wait_ge(S.a, 1)
    P.wait_ge(S.cz2, 1)
    P.wait_ge(S.cz3a, 1)
    P.wait_ge(S.cz3b, 1)
    for c in range(2):
        for q in range(2):
            lo = HALF * c + PIECE * q
            P.wait_ge(S["dg%d%d" % (c, q)], 1)
            P.matmul(scal(c, q), T.ones[:], T.dg[:, lo:lo + PIECE], True, True).then_inc(S["S%d%d" % (c, q)], 1)
    P.wait_ge(S.qv, 1)
    for c in range(2):
        P.wait_ge(S["cz%d" % c], 1)
        P.wait_ge(S["qh%d" % c], 1)
        P.matmul_mx(zb(c, 0, HALF), T.w2q[:, 0:128], T.w2s[:, 0:128],
                    T.hq[:, HALF * c:HALF * c + HALF], T.hs[:, HALF * c:HALF * c + HALF], True, False)
    for c in range(2):
        P.wait_ge(S["arr%d" % c], 2 * eng)
        P.matmul_mx(zb(c, 0, HALF), T.w2q[:, 128:256], T.w2s[:, 128:256],
                    T.rq[:, HALF * c:HALF * c + HALF], T.rs[:, HALF * c:HALF * c + HALF], False, True).then_inc(S["y%d" % c], 1)

    A.wait_ge(S.z0, 1)
    A.activation(sb(T.sq, 0), zb(0), AF.Square).then_inc(S.sq0, 1)
    A.activation(sb(T.zs, 0), zb(0), AF.Copy).then_inc(S.cz0, 1)
    A.wait_ge(S.z1, 1)
    A.activation(sb(T.sq, 1), zb(1), AF.Square).then_inc(S.sq1, 1)
    A.wait_ge(S.A, 2)
    A.activation(pair(RA), T.pS[:, 0:2], AF.Sqrt, bias=EPS).then_inc(S.ra, 1)
    A.activation(pair(AA), T.pS[:, 0:2], AF.Identity, bias=EPS).then_inc(S.a, 1)
    for c, t in HALVES:
        A.wait_ge(S["z3" + t], 1)
        A.activation(sb(T.sq, 3, HALF * c, HALF * c + HALF), z3(c), AF.Square).then_inc(S["sq3" + t], 1)
    A.wait_ge(S.k, 1)
    A.wait_ge(S.ident, 1)
    A.activation(T.idk[:], T.ident[:], AF.Identity, scale=col(K, 1)).then_inc(S.idk, 1)
    A.wait_ge(S.k2, 1)
    A.wait_ge(S.c2, 1)
    for c in range(2):
        A.wait_ge(S["R%d" % c], 1)
        A.activation(col(RQ, c), T.pr[:, 512 * c:512 * c + 1], AF.Sqrt, bias=col(C2, c), scale=col(K2, c)).then_inc(S["rq%d" % c], 1)
    A.wait_ge(S.idk, 1)
    A.wait_ge(S.iq1, 1)
    for q in range(2):
        A.activation(T.dg[:, HALF + PIECE * q:HALF + PIECE * q + PIECE], T.idk[:, PIECE * q:PIECE * q + PIECE], AF.Identity,
                     scale=col(IQ, 1)).then_inc(S["dg1%d" % q], 1)
    for c in range(2):
        lo, hi = HALF * c, HALF * c + HALF
        A.wait_ge(S["y%d" % c], 1)
        A.activation(T.yb[:, lo:hi], zb(c, 0, HALF), AF.Copy).then_inc(S["yc%d" % c], 1)
        A.wait_ge(S["yc%d" % c], 1)
        A.dma_start(T.y[:, lo:hi], T.yb[:, lo:hi]).then_inc(S["st%d" % c], 16)
    A.wait_ge(S.st0, 16)
    A.wait_ge(S.st1, 16)

    g.wait_ge(S.ones, 1)
    g.affine_select(T.ident[:], T.ones[:], [[-1, 128]], OP.is_equal, 0.0, 0, 1).then_inc(S.ident, 1)
    for c in range(2):
        lo, hi = HALF * c, HALF * c + HALF
        g.wait_ge(S["qh%d" % c], 1)
        g.remote_dma(T.rq[:, lo:hi].bitcast(dt.uint8), T.hq[:, lo:hi].bitcast(dt.uint8), S["arr%d" % c], S.sent, pid, rid, mask)
        g.remote_dma(T.rs[:, lo:hi], T.hs[:, lo:hi], S["arr%d" % c], S.sent, pid, rid, mask)
    g.wait_ge(S.sent, 4 * eng)

    Y.wait_ge(S.hm0, 8)
    Y.wait_ge(S.hm1, 8)
    Y.wait_ge(S.sent, 4 * eng)
    Y.dma_start(T.h[:], T.hb[:]).then_inc(S.hst, 16)
    Y.wait_ge(S.hst, 16)
